import numpy as np
import ml_dtypes


def mxq(x, axis, fmt="e4m3"):
    dtype, down = {"e4m3": (ml_dtypes.float8_e4m3fn, 7), "e5m2": (ml_dtypes.float8_e5m2, 14)}[fmt]
    v = np.moveaxis(np.asarray(x, np.float32).astype(ml_dtypes.bfloat16).astype(np.float64), axis, -1)
    blocks = v.reshape(v.shape[:-1] + (-1, 32))
    amax = np.abs(blocks).max(-1, keepdims=True)
    byte = np.maximum(np.where(amax > 0, np.frexp(amax)[1] - 1 + 127, 0) - down, 1)
    scale = np.exp2(byte - 127.0)
    codes = (blocks / scale).astype(np.float32).astype(dtype).astype(np.float64)
    return np.moveaxis((codes * scale).reshape(v.shape), -1, axis)


WIDE = False


def mx_kscale(k):
    if not WIDE:
        return np.ones(k)
    levels = np.array([10, -10, 5, -5, 0])
    if k % 512:
        return np.exp2(np.random.permutation(np.resize(levels, k // 32))).repeat(32)
    a = np.empty((k // 512, 16))
    for p in range(k // 512):
        a[p, :8] = np.random.permutation(np.resize(levels, 8))
        for g in range(8):
            far = levels[np.abs(levels - a[p, g]) >= 10]
            a[p, g + 8] = far[np.random.randint(len(far))]
    return np.exp2(a.ravel()).repeat(32)


def f64(x):
    return np.asarray(x).astype(np.float64)


def striped(idx):
    return np.tile(idx.reshape(-1, 16).T, (8, 1)).astype(np.uint16)


def unstriped(offs):
    return offs[:16].T.reshape(-1).astype(np.int64)


E2M1 = np.array([0.0, 0.5, 1.0, 1.5, 2.0, 3.0, 4.0, 6.0, -0.0, -0.5, -1.0, -1.5, -2.0, -3.0, -4.0, -6.0])


def pack_weight(w, fmt):
    k, n = w.shape
    w = f64(np.asarray(w, np.float32).astype(ml_dtypes.bfloat16)).reshape(k // 32, 32, n)
    amax = np.abs(w).max(1)
    if fmt == "e4m3":
        byte = np.frexp(amax)[1] - 1 + 127 - 7
    else:
        mant, ex = np.frexp(amax / 6.0)
        byte = np.where(mant > 0.5, ex, ex - 1) + 127
    byte = np.clip(np.where(amax > 0, byte, 1), 1, 254)
    scaled = (w * np.exp2(127.0 - byte)[:, None, :]).reshape(k, n).astype(np.float32)
    by_word = np.ascontiguousarray(scaled.reshape(k // 512, 128, 4, n).transpose(0, 1, 3, 2))
    if fmt == "e4m3":
        words = by_word.astype(ml_dtypes.float8_e4m3fn).view(np.uint8)
    else:
        c = by_word.astype(ml_dtypes.float4_e2m1fn).view(np.uint8) & 0xF
        words = (c[..., 0::2] | (c[..., 1::2] << 4)).reshape(k // 512, 128, 2 * n)
    return np.ascontiguousarray(words), np.ascontiguousarray(byte.astype(np.uint8).reshape(k // 512, 16, n))


def unpack_weight(words, scales, fmt):
    g, _, n = scales.shape
    words = np.ascontiguousarray(words).reshape(g, 128, n, -1)
    if fmt == "e4m3":
        vals = words.view(ml_dtypes.float8_e4m3fn).astype(np.float64)
    else:
        nib = np.empty((g, 128, n, 4), np.uint8)
        nib[..., 0::2] = words & 0xF
        nib[..., 1::2] = words >> 4
        vals = E2M1[nib]
    vals = vals * np.repeat(np.exp2(scales.astype(np.float64) - 127.0), 8, axis=1)[..., None]
    return vals.transpose(0, 1, 3, 2).reshape(g * 512, n)


def gelu(v):
    return 0.5 * v * (1.0 + np.tanh(np.sqrt(2.0 / np.pi) * (v + 0.044715 * v**3)))


K, KA, KB, H, T, S, T2, P, T3, S2 = 1536, 512, 1024, 1024, 4096, 1024, 2048, 512, 2048, 1024


def setup_inputs():
    n = np.random.standard_normal
    s = mx_kscale(K)[:, None]
    u = mx_kscale(H)[:, None]
    tab_words, tab_scales = pack_weight(n((K, T)) * s, "e4m3")
    tab2_words, tab2_scales = pack_weight(n((H, T3)) / np.sqrt(H) / u, "e4m3")
    w4_words, w4_scales = pack_weight(1.8 * n((KB, H)) / np.sqrt(K) / s[KA:], "e2m1")
    return {
        "tab_words": tab_words, "tab_scales": tab_scales,
        "w1": (1.8 * n((KA, H)) / np.sqrt(K) / s[:KA]).astype(np.float32),
        "w4_words": w4_words, "w4_scales": w4_scales,
        "b1": (0.7 * n(H)).astype(np.float32),
        "gain": (np.random.uniform(0.8, 2.0, H) * u[:, 0]).astype(np.float32),
        "page0": (n((H, T2)) * u).astype(np.float32),
        "wgs": np.exp(0.3 * n((128, S))).astype(np.float32),
        "low": (0.5 * n(H) * u[:, 0]).astype(np.float32),
        "tab2_words": tab2_words, "tab2_scales": tab2_scales,
        "cand": np.exp(0.4 * n(S2)).astype(np.float32),
        "pagedist": (0.5 * n((S2, P))).astype(np.float32),
        "offs": striped(np.random.permutation(T)[:S]),
        "offs2": striped(np.random.permutation(T3)[:S2]),
        "offs3": striped(np.random.permutation(T2)[:S]),
        "offs4": striped(np.random.permutation(T2)[:P]),
    }


def reference(tab_words, tab_scales, w1, w4_words, w4_scales, b1, gain, page0, wgs, low,
              tab2_words, tab2_scales, cand, pagedist, offs, offs2, offs3, offs4):
    v = unpack_weight(tab_words, tab_scales, "e4m3")[:, unstriped(offs)]
    v2 = unpack_weight(tab2_words, tab2_scales, "e4m3")[:, unstriped(offs2)]
    w4 = unpack_weight(w4_words, w4_scales, "e2m1")
    y = mxq(f64(w1), 0, "e4m3").T @ v[:KA] + w4.T @ v[KA:]
    h = np.tanh(y + f64(b1)[:, None]) * f64(gain)[:, None]
    page = f64(page0).copy()
    page[:, unstriped(offs3)] = np.tile(f64(wgs), (H // 128, 1)) * h
    x = np.maximum(page[:, unstriped(offs4)], f64(low)[:, None])
    e = v2.T @ mxq(x, 0, "e4m3")
    return e * f64(cand)[:, None] + f64(pagedist)

@@ -1,0 +1,295 @@
+from contextlib import ExitStack
+
+import concourse.mybir as mybir
+
+K, KA, KB, H, T, S, T2, NP, T3, S2 = 1536, 512, 1024, 1024, 4096, 1024, 2048, 512, 2048, 1024
+FLOPS = 2 * K * H * S + 2 * H * S2 * NP
+
+F32 = mybir.dt.float32
+BF16 = mybir.dt.bfloat16
+I32 = mybir.dt.int32
+U32 = mybir.dt.uint32
+U16 = mybir.dt.uint16
+U8 = mybir.dt.uint8
+FP8X4 = mybir.dt.float8_e4m3fn_x4
+FP4X4 = mybir.dt.float4_e2m1fn_x4
+ALU = mybir.AluOpType
+ACT = mybir.ActivationFunctionType
+
+P = 128
+PACK = 4
+BANK = 512
+QUADS = 4
+ROW_TILES = H // P
+SPLIT = 48
+
+
+def tile_list_microfilm_article_linker_kernel(
+    tc, tab_words, tab_scales, w1, w4_words, w4_scales, b1, gain, page0, wgs, low,
+    tab2_words, tab2_scales, cand, pagedist, offs, offs2, offs3, offs4, out,
+):
+    nc = tc.nc
+    with ExitStack() as ctx:
+        lists = ctx.enter_context(tc.tile_pool(name="lists", bufs=1))
+        keep = ctx.enter_context(tc.tile_pool(name="keep", bufs=1))
+        shared = ctx.enter_context(tc.tile_pool(name="shared", bufs=1))
+        ring = ctx.enter_context(tc.tile_pool(name="ring", bufs=3))
+        psum = ctx.enter_context(tc.psum_pool(name="psum", bufs=1))
+
+        idx = lists.tile([P, S // 16], U16, name="idx")
+        idx2 = lists.tile([P, S2 // 16], U16, name="idx2")
+        idx3 = lists.tile([P, S // 16], U16, name="idx3")
+        idx4 = lists.tile([P, NP // 16], U16, name="idx4")
+        banks = [psum.tile([P, BANK], F32, name="bank%d" % i) for i in range(8)]
+
+        tab_sb = [shared.tile([P, T], I32, name="tab%d" % a, offset=4 * T * ((a + 2) % 3)) for a in range(3)]
+        tab_sc = keep.tile([P, T], U8, name="tab_sc")
+        v_words = [keep.tile([P, S], U32, name="v_words%d" % a, align_bytes=64) for a in range(3)]
+        v_sc_rows = keep.tile([P, S], U8, name="v_sc_rows", align_bytes=64)
+        v_sc = keep.tile([P, 3 * S], U8, name="v_sc", align_bytes=64)
+        w4_raw = keep.tile([P, 2 * 2 * H], U8, name="w4_raw", align_bytes=64)
+        w4_sb = keep.tile([P, 2 * 2 * H], U8, name="w4_sb", align_bytes=64)
+        w4s_raw = keep.tile([P, 2 * H], U8, name="w4s_raw", align_bytes=64)
+        w4s_sb = keep.tile([P, 2 * H], U8, name="w4s_sb", align_bytes=64)
+        w1_raw = [keep.tile([P, PACK, BANK], F32, name="w1_raw%d" % b, tag="stage%d" % b) for b in range(2)]
+        w1_bf = [keep.tile([P, PACK * BANK], BF16, name="w1_bf%d" % b, tag="bf%d" % b, align_bytes=64) for b in range(2)]
+        w1_q = [keep.tile([P, BANK], U32, name="w1_q%d" % b, align_bytes=64) for b in range(2)]
+        w1_sc = [keep.tile([P, BANK], U8, name="w1_sc%d" % b, align_bytes=64) for b in range(2)]
+        b1_sb = keep.tile([P, 2, PACK], F32, name="b1_sb")
+        gain_sb = keep.tile([P, 2, PACK], F32, name="gain_sb")
+        cand_sb = keep.tile([P, S2 // P], F32, name="cand_sb")
+        wgs_sb = [keep.tile([P, S], F32, name="wgs%d" % t) for t in range(PACK)]
+        tab2_sb = [keep.tile([P, T3], I32, name="tab2_%d" % a) for a in range(2)]
+        tab2_sc = keep.tile([P, T3], U8, name="tab2_sc")
+        v2_words = [keep.tile([P, S2], U32, name="v2_words%d" % a, align_bytes=64) for a in range(2)]
+        v2_sc = keep.tile([P, S2], U8, name="v2_sc", align_bytes=64)
+        h = [keep.tile([P, S], F32, name="h%d" % i) for i in range(ROW_TILES)]
+        x_planes = [keep.tile([P, PACK, NP], BF16, name="x_planes%d" % b, align_bytes=64) for b in range(2)]
+        x_q = [keep.tile([P, NP], U32, name="x_q%d" % b, align_bytes=64) for b in range(2)]
+        x_sc = [keep.tile([P, NP], U8, name="x_sc%d" % b, align_bytes=64) for b in range(2)]
+
+        for plane in (w4s_raw[:], tab2_sc[:], tab_sc[0:80, :], v_sc[:]):
+            nc.vector.memset(plane.bitcast(I32), 0)
+
+        def load_words(dst, words, a):
+            nc.sync.dma_start(out=dst[:], in_=words[a].rearrange("p t i -> p (t i)").bitcast(I32))
+
+        def load_wgs(t, cols):
+            rows = wgs.rearrange("(q t) s -> t q s", t=PACK)[t]
+            for g in (0, 2, 1, 3):
+                nc.sync.dma_start(out=wgs_sb[t][32 * g : 32 * (g + 1), cols], in_=rows[:, cols])
+
+        def load_w1(b):
+            rows = w1.rearrange("(p j) c -> p j c", j=PACK)
+            nc.sync.dma_start(out=w1_raw[b][:], in_=rows[:, :, b * BANK : (b + 1) * BANK])
+
+        pages = []
+
+        def load_page(i):
+            b, t = divmod(i, PACK)
+            if i < 2:
+                page = keep.tile([P, T2], F32, name="page%d" % i)
+            else:
+                page = shared.tile([P, T2], F32, name="page%d" % i, offset=(4 * T2 + 64) * (i - 2))
+            rows = page0.rearrange("(b p t) n -> b t p n", b=2, t=PACK)[b, t]
+            nc.sync.dma_start(out=page[:], in_=rows)
+            pages.append(page)
+
+        low_sb = {}
+
+        def load_low(i, count):
+            b, t = divmod(i, PACK)
+            if i == 0:
+                col = keep.tile([P, count], F32, name="low0")
+            else:
+                col = shared.tile([P, count], F32, name="low%d" % i, offset=(4 * T2 + 64) * min(i - 1, 4) + 4 * T2 + (32 if i == 6 else 0))
+            with nc.allow_non_contiguous_dma(reason="one value a partition"):
+                nc.sync.dma_start(out=col[:], in_=low.rearrange("(b p t) -> b p t", b=2, t=PACK)[b, :, t : t + count])
+            for j in range(count):
+                low_sb[i + j] = col[:, j : j + 1]
+
+        def quantise_w1(b):
+            nc.scalar.copy(
+                out=w1_bf[b][:].rearrange("p (t m j) -> p m t j", t=PACK, j=PACK),
+                in_=w1_raw[b][:].rearrange("p j (m t) -> p m t j", t=PACK),
+            )
+            nc.vector.quantize_mx(out=w1_q[b][:].bitcast(FP8X4), scales=w1_sc[b][:], in_=w1_bf[b][:])
+
+        def gather_words(dst, src, offsets, lo, hi):
+            nc.vector.tensor_copy(dst[:, lo:hi], src[:].bitcast(U32).indirect(offsets[:, lo // 16 : hi // 16]))
+
+        scale_rows = tab_scales.bitcast(I32).rearrange("a q n -> (a q) n")
+        nc.scalar.dma_start(out=tab_sc[96:128, :].bitcast(I32), in_=scale_rows[16:48, :])
+        nc.scalar.dma_start(out=tab_sc[80:96, :].bitcast(I32), in_=scale_rows[0:16, :])
+        nc.sync.dma_start(idx[:], offs)
+        nc.sync.dma_start(
+            out=w4_raw[:].bitcast(I32).rearrange("p (a c) -> p a c", a=2),
+            in_=w4_words.bitcast(I32).rearrange("a p c -> p a c"),
+        )
+        load_words(tab_sb[1], tab_words, 1)
+        for q in range(QUADS):
+            nc.scalar.dma_start(
+                out=w4s_raw[32 * q : 32 * q + 4, :].bitcast(I32).rearrange("p (a c) -> p a c", a=2),
+                in_=w4_scales[:, 4 * q : 4 * q + 4, :].bitcast(I32).rearrange("a r c -> r a c"),
+            )
+        for q in range(QUADS):
+            nc.gpsimd.dma_start(
+                out=tab2_sc[32 * q : 32 * q + 8, :].bitcast(I32),
+                in_=tab2_scales[:, 4 * q : 4 * q + 4, :].bitcast(I32),
+            )
+        load_w1(0)
+        nc.sync.dma_start(idx2[:], offs2)
+        load_words(tab_sb[2], tab_words, 2)
+        for vec, dst in ((b1, b1_sb), (gain, gain_sb)):
+            nc.sync.dma_start(out=dst[:], in_=vec.rearrange("(b p t) -> p b t", b=2, t=PACK))
+        load_words(tab_sb[0], tab_words, 0)
+        load_page(0)
+        nc.sync.dma_start(idx3[:], offs3)
+        load_wgs(0, slice(0, BANK))
+        load_wgs(0, slice(BANK, S))
+        nc.sync.dma_start(idx4[:], offs4)
+
+        nc.vector.tensor_copy(v_sc_rows[:], tab_sc[:].indirect(idx[:]))
+        for a in (1, 2, 0):
+            first = 80 + 16 * a
+            for q in range(QUADS):
+                nc.gpsimd.dma_start(
+                    out=v_sc[32 * q : 32 * q + 4, a * S : (a + 1) * S].bitcast(I32),
+                    in_=v_sc_rows[first + 4 * q : first + 4 * q + 4, :].bitcast(I32),
+                )
+        nc.vector.tensor_copy(
+            out=w4_sb[:].bitcast(U16).rearrange("p (g t u i) -> p g u t i", g=4, t=PACK, i=8),
+            in_=w4_raw[:].bitcast(U16).rearrange("p (g u i t) -> p g u t i", g=4, t=PACK, i=8),
+        )
+        nc.vector.tensor_copy(
+            out=w4s_sb[:].rearrange("p (g t u i) -> p g u t i", g=4, t=PACK, i=16),
+            in_=w4s_raw[:].rearrange("p (g u i t) -> p g u t i", g=4, t=PACK, i=16),
+        )
+        gather_words(v_words[1], tab_sb[1], idx, 0, S)
+        quantise_w1(0)
+        gather_words(v_words[2], tab_sb[2], idx, 0, S)
+        nc.vector.tensor_copy(v2_sc[:], tab2_sc[:].indirect(idx2[:]))
+        gather_words(v_words[0], tab_sb[0], idx, 0, BANK)
+        gather_words(v_words[0], tab_sb[0], idx, BANK, S)
+
+        load_page(1)
+        load_wgs(1, slice(0, S))
+        load_w1(1)
+        load_low(0, 1)
+        load_words(tab2_sb[0], tab2_words, 0)
+        load_words(tab2_sb[1], tab2_words, 1)
+        load_wgs(2, slice(0, S))
+        load_wgs(3, slice(0, S))
+        with nc.allow_non_contiguous_dma(reason="one factor a partition"):
+            nc.sync.dma_start(out=cand_sb[:], in_=cand.rearrange("(c p) -> p c", p=P))
+        for i in range(2, ROW_TILES):
+            load_page(i)
+            load_low(i - 1, 2 if i == ROW_TILES - 1 else 1)
+        quantise_w1(1)
+
+        def first_product(i):
+            b, t = divmod(i, PACK)
+            for half in range(2):
+                bank = banks[(2 * i + half) % 8]
+                cols = slice(half * BANK, (half + 1) * BANK)
+                for a in range(2):
+                    c0 = a * H + i * P
+                    nc.tensor.matmul_mx(
+                        out=bank[:],
+                        lhsT=w4_sb[:, 2 * c0 : 2 * (c0 + P)].bitcast(FP4X4),
+                        lhsT_scale=w4s_sb[:, c0 : c0 + P],
+                        rhs=v_words[1 + a][:, cols].bitcast(FP8X4),
+                        rhs_scale=v_sc[:, (1 + a) * S + half * BANK : (1 + a) * S + (half + 1) * BANK],
+                        start=(a == 0),
+                        stop=False,
+                    )
+                nc.tensor.matmul_mx(
+                    out=bank[:],
+                    lhsT=w1_q[b][:, t * P : (t + 1) * P].bitcast(FP8X4),
+                    lhsT_scale=w1_sc[b][:, t * P : (t + 1) * P],
+                    rhs=v_words[0][:, cols].bitcast(FP8X4),
+                    rhs_scale=v_sc[:, cols],
+                    start=False,
+                    stop=True,
+                )
+                level = ring.tile([P, BANK], F32, name="level")
+                nc.scalar.activation(out=level[:], in_=bank[:], func=ACT.Tanh, bias=b1_sb[:, b, t : t + 1])
+                nc.scalar.activation(out=h[i][:, cols], in_=level[:], func=ACT.Copy, scale=gain_sb[:, b, t : t + 1])
+
+        def put(i, lo, hi):
+            nc.vector.tensor_tensor(
+                pages[i][:].indirect(idx3[:, lo // 16 : hi // 16]),
+                h[i][:, lo:hi], wgs_sb[i % PACK][:, lo:hi], ALU.mult,
+            )
+
+        picked = {}
+
+        def fetch(i, lo, hi):
+            if lo == 0:
+                picked[i] = ring.tile([P, NP], F32, name="picked")
+            nc.vector.tensor_copy(picked[i][:, lo:hi], pages[i][:].indirect(idx4[:, lo // 16 : hi // 16]))
+
+        def raise_to_low(i, lo, hi):
+            b, t = divmod(i, PACK)
+            nc.vector.tensor_scalar(
+                out=x_planes[b][:, t, lo:hi], in0=picked[i][:, lo:hi], scalar1=low_sb[i], scalar2=None, op0=ALU.max,
+            )
+
+        def second_pass(b):
+            x_bf = keep.tile([P, NP, PACK], BF16, name="x_bf%d" % b, tag="bf%d" % b, align_bytes=64)
+            dst = x_bf[:].rearrange("p (c i) t -> p c t i", i=4)
+            src = x_planes[b][:].rearrange("p t (c i) -> p c t i", i=4)
+            if b == 0:
+                nc.scalar.copy(out=dst, in_=src)
+            else:
+                nc.scalar.copy(out=dst[:, :SPLIT], in_=src[:, :SPLIT])
+                nc.vector.tensor_copy(out=dst[:, SPLIT:], in_=src[:, SPLIT:])
+            nc.vector.quantize_mx(
+                out=x_q[b][:].bitcast(FP8X4), scales=x_sc[b][:], in_=x_bf[:].rearrange("p n t -> p (n t)"),
+            )
+            for c in range(S2 // P):
+                cols = slice(c * P, (c + 1) * P)
+                nc.tensor.matmul_mx(
+                    out=banks[c][:],
+                    lhsT=v2_words[b][:, cols].bitcast(FP8X4),
+                    lhsT_scale=v2_sc[4 * b : P, cols],
+                    rhs=x_q[b][:].bitcast(FP8X4),
+                    rhs_scale=x_sc[b][:],
+                    start=(b == 0),
+                    stop=(b == 1),
+                )
+
+        for i in range(ROW_TILES):
+            first_product(i)
+
+        score = []
+        for u in range(2):
+            part = keep.tile([P, PACK, NP], F32, name="score%d" % u, tag="stage%d" % u)
+            nc.sync.dma_start(out=part[:], in_=pagedist.rearrange("(u c p) n -> u p c n", u=2, p=P)[u])
+            score.append(part)
+
+        put(0, 0, BANK)
+        put(0, BANK, S)
+        fetch(0, 0, NP)
+        for i in range(1, ROW_TILES):
+            put(i, 0, S)
+            raise_to_low(i - 1, 0, NP)
+            if i < ROW_TILES - 1:
+                fetch(i, 0, NP)
+            if i <= 2:
+                gather_words(v2_words[i - 1], tab2_sb[i - 1], idx2, 0, S2)
+            if i == PACK:
+                second_pass(0)
+        last = ROW_TILES - 1
+        fetch(last, 0, NP // 2)
+        fetch(last, NP // 2, NP)
+        raise_to_low(last, 0, NP // 2)
+        raise_to_low(last, NP // 2, NP)
+        second_pass(1)
+
+        for c in range(S2 // P):
+            part = score[c // PACK][:, c % PACK, :]
+            nc.vector.scalar_tensor_tensor(
+                out=part, in0=banks[c][:], scalar=cand_sb[:, c : c + 1], in1=part, op0=ALU.mult, op1=ALU.add,
+            )
+            nc.sync.dma_start(out=out[c * P : (c + 1) * P, :], in_=part)

@@ -23,6 +23,19 @@ QUADS = 4
 ROW_TILES = H // P
 SPLIT = 48
 
+KIB = 1024
+SLOT = 32
+AT_TAB = {1: 0, 2: 16 * KIB, 0: 32 * KIB}
+AT_WGS = {0: 57600, 1: 0, 2: 12 * KIB + SLOT, 3: 86336 + SLOT}
+AT_W1 = {0: 73984, 1: 4 * KIB}
+AT_PAGE = {0: 49408, 1: 61696, 2: 16416, 3: 24640, 4: 32864, 5: 41120, 6: 69888, 7: 78144}
+AT_LOW = {0: 12 * KIB, 1: 24608, 2: 32832, 3: 41056, 4: 41088, 5: 78080, 6: 78112}
+AT_TAB2 = {0: 69888, 1: 78080}
+AT_TAB_SC = 47104
+AT_W4 = 59648
+AT_W1_BF = 86336
+AT_CAND = 86336
+
 
 def tile_list_microfilm_article_linker_kernel(
     tc, tab_words, tab_scales, w1, w4_words, w4_scales, b1, gain, page0, wgs, low,
@@ -42,24 +55,27 @@ def tile_list_microfilm_article_linker_kernel(
         idx4 = lists.tile([P, NP // 16], U16, name="idx4")
         banks = [psum.tile([P, BANK], F32, name="bank%d" % i) for i in range(8)]
 
-        tab_sb = [shared.tile([P, T], I32, name="tab%d" % a, offset=4 * T * ((a + 2) % 3)) for a in range(3)]
-        tab_sc = keep.tile([P, T], U8, name="tab_sc")
+        tab_sb = [shared.tile([P, T], I32, name="tab%d" % a, offset=AT_TAB[a]) for a in range(3)]
+        tab_sc = shared.tile([P, T], U8, name="tab_sc", offset=AT_TAB_SC)
         v_words = [keep.tile([P, S], U32, name="v_words%d" % a, align_bytes=64) for a in range(3)]
         v_sc_rows = keep.tile([P, S], U8, name="v_sc_rows", align_bytes=64)
         v_sc = keep.tile([P, 3 * S], U8, name="v_sc", align_bytes=64)
-        w4_raw = keep.tile([P, 2 * 2 * H], U8, name="w4_raw", align_bytes=64)
+        w4_raw = shared.tile([P, 2 * 2 * H], U8, name="w4_raw", offset=AT_W4)
         w4_sb = keep.tile([P, 2 * 2 * H], U8, name="w4_sb", align_bytes=64)
         w4s_raw = keep.tile([P, 2 * H], U8, name="w4s_raw", align_bytes=64)
         w4s_sb = keep.tile([P, 2 * H], U8, name="w4s_sb", align_bytes=64)
-        w1_raw = [keep.tile([P, PACK, BANK], F32, name="w1_raw%d" % b, tag="stage%d" % b) for b in range(2)]
-        w1_bf = [keep.tile([P, PACK * BANK], BF16, name="w1_bf%d" % b, tag="bf%d" % b, align_bytes=64) for b in range(2)]
+        w1_raw = [shared.tile([P, PACK, BANK], F32, name="w1_raw%d" % b, offset=AT_W1[b]) for b in range(2)]
+        w1_bf = [
+            shared.tile([P, PACK * BANK], BF16, name="w1_bf0", align_bytes=64, offset=AT_W1_BF),
+            keep.tile([P, PACK * BANK], BF16, name="w1_bf1", align_bytes=64),
+        ]
         w1_q = [keep.tile([P, BANK], U32, name="w1_q%d" % b, align_bytes=64) for b in range(2)]
         w1_sc = [keep.tile([P, BANK], U8, name="w1_sc%d" % b, align_bytes=64) for b in range(2)]
         b1_sb = keep.tile([P, 2, PACK], F32, name="b1_sb")
         gain_sb = keep.tile([P, 2, PACK], F32, name="gain_sb")
-        cand_sb = keep.tile([P, S2 // P], F32, name="cand_sb")
-        wgs_sb = [keep.tile([P, S], F32, name="wgs%d" % t) for t in range(PACK)]
-        tab2_sb = [keep.tile([P, T3], I32, name="tab2_%d" % a) for a in range(2)]
+        cand_sb = shared.tile([P, S2 // P], F32, name="cand_sb", offset=AT_CAND)
+        wgs_sb = [shared.tile([P, S], F32, name="wgs%d" % t, offset=AT_WGS[t]) for t in range(PACK)]
+        tab2_sb = [shared.tile([P, T3], I32, name="tab2_%d" % a, offset=AT_TAB2[a]) for a in range(2)]
         tab2_sc = keep.tile([P, T3], U8, name="tab2_sc")
         v2_words = [keep.tile([P, S2], U32, name="v2_words%d" % a, align_bytes=64) for a in range(2)]
         v2_sc = keep.tile([P, S2], U8, name="v2_sc", align_bytes=64)
@@ -68,7 +84,7 @@ def tile_list_microfilm_article_linker_kernel(
         x_q = [keep.tile([P, NP], U32, name="x_q%d" % b, align_bytes=64) for b in range(2)]
         x_sc = [keep.tile([P, NP], U8, name="x_sc%d" % b, align_bytes=64) for b in range(2)]
 
-        for plane in (w4s_raw[:], tab2_sc[:], tab_sc[0:80, :], v_sc[:]):
+        for plane in (tab_sc[0:80, :], w4s_raw[:], v_sc[:], tab2_sc[:]):
             nc.vector.memset(plane.bitcast(I32), 0)
 
         def load_words(dst, words, a):
@@ -87,10 +103,7 @@ def tile_list_microfilm_article_linker_kernel(
 
         def load_page(i):
             b, t = divmod(i, PACK)
-            if i < 2:
-                page = keep.tile([P, T2], F32, name="page%d" % i)
-            else:
-                page = shared.tile([P, T2], F32, name="page%d" % i, offset=(4 * T2 + 64) * (i - 2))
+            page = shared.tile([P, T2], F32, name="page%d" % i, offset=AT_PAGE[i])
             rows = page0.rearrange("(b p t) n -> b t p n", b=2, t=PACK)[b, t]
             nc.sync.dma_start(out=page[:], in_=rows)
             pages.append(page)
@@ -99,10 +112,7 @@ def tile_list_microfilm_article_linker_kernel(
 
         def load_low(i, count):
             b, t = divmod(i, PACK)
-            if i == 0:
-                col = keep.tile([P, count], F32, name="low0")
-            else:
-                col = shared.tile([P, count], F32, name="low%d" % i, offset=(4 * T2 + 64) * min(i - 1, 4) + 4 * T2 + (32 if i == 6 else 0))
+            col = shared.tile([P, count], F32, name="low%d" % i, offset=AT_LOW[i])
             with nc.allow_non_contiguous_dma(reason="one value a partition"):
                 nc.sync.dma_start(out=col[:], in_=low.rearrange("(b p t) -> b p t", b=2, t=PACK)[b, :, t : t + count])
             for j in range(count):
@@ -119,48 +129,50 @@ def tile_list_microfilm_article_linker_kernel(
             nc.vector.tensor_copy(dst[:, lo:hi], src[:].bitcast(U32).indirect(offsets[:, lo // 16 : hi // 16]))
 
         scale_rows = tab_scales.bitcast(I32).rearrange("a q n -> (a q) n")
-        nc.scalar.dma_start(out=tab_sc[96:128, :].bitcast(I32), in_=scale_rows[16:48, :])
-        nc.scalar.dma_start(out=tab_sc[80:96, :].bitcast(I32), in_=scale_rows[0:16, :])
         nc.sync.dma_start(idx[:], offs)
+        nc.sync.dma_start(out=tab_sc[96:128, :].bitcast(I32), in_=scale_rows[16:48, :])
+        nc.sync.dma_start(out=tab_sc[80:96, :].bitcast(I32), in_=scale_rows[0:16, :])
         nc.sync.dma_start(
             out=w4_raw[:].bitcast(I32).rearrange("p (a c) -> p a c", a=2),
             in_=w4_words.bitcast(I32).rearrange("a p c -> p a c"),
         )
+        nc.sync.dma_start(idx2[:], offs2)
+        nc.sync.dma_start(idx3[:], offs3)
+        nc.sync.dma_start(idx4[:], offs4)
         load_words(tab_sb[1], tab_words, 1)
         for q in range(QUADS):
-            nc.scalar.dma_start(
+            nc.gpsimd.dma_start(
                 out=w4s_raw[32 * q : 32 * q + 4, :].bitcast(I32).rearrange("p (a c) -> p a c", a=2),
                 in_=w4_scales[:, 4 * q : 4 * q + 4, :].bitcast(I32).rearrange("a r c -> r a c"),
             )
+        for vec, dst in ((b1, b1_sb), (gain, gain_sb)):
+            nc.gpsimd.dma_start(out=dst[:], in_=vec.rearrange("(b p t) -> p b t", b=2, t=PACK))
         for q in range(QUADS):
             nc.gpsimd.dma_start(
                 out=tab2_sc[32 * q : 32 * q + 8, :].bitcast(I32),
                 in_=tab2_scales[:, 4 * q : 4 * q + 4, :].bitcast(I32),
             )
         load_w1(0)
-        nc.sync.dma_start(idx2[:], offs2)
         load_words(tab_sb[2], tab_words, 2)
-        for vec, dst in ((b1, b1_sb), (gain, gain_sb)):
-            nc.sync.dma_start(out=dst[:], in_=vec.rearrange("(b p t) -> p b t", b=2, t=PACK))
-        load_words(tab_sb[0], tab_words, 0)
-        load_page(0)
-        nc.sync.dma_start(idx3[:], offs3)
-        load_wgs(0, slice(0, BANK))
-        load_wgs(0, slice(BANK, S))
-        nc.sync.dma_start(idx4[:], offs4)
 
         nc.vector.tensor_copy(v_sc_rows[:], tab_sc[:].indirect(idx[:]))
-        for a in (1, 2, 0):
-            first = 80 + 16 * a
-            for q in range(QUADS):
-                nc.gpsimd.dma_start(
-                    out=v_sc[32 * q : 32 * q + 4, a * S : (a + 1) * S].bitcast(I32),
-                    in_=v_sc_rows[first + 4 * q : first + 4 * q + 4, :].bitcast(I32),
-                )
+        moves = [(a, q) for a in (1, 2, 0) for q in range(QUADS)]
+        for n, (a, q) in enumerate(moves):
+            if n == len(moves) // 2:
+                load_words(tab_sb[0], tab_words, 0)
+            first = 80 + 16 * a + 4 * q
+            nc.sync.dma_start(
+                out=v_sc[32 * q : 32 * q + 4, a * S : (a + 1) * S].bitcast(I32),
+                in_=v_sc_rows[first : first + 4, :].bitcast(I32),
+            )
         nc.vector.tensor_copy(
             out=w4_sb[:].bitcast(U16).rearrange("p (g t u i) -> p g u t i", g=4, t=PACK, i=8),
             in_=w4_raw[:].bitcast(U16).rearrange("p (g u i t) -> p g u t i", g=4, t=PACK, i=8),
         )
+        load_page(0)
+        load_wgs(0, slice(0, S))
+        load_page(1)
+
         nc.vector.tensor_copy(
             out=w4s_sb[:].rearrange("p (g t u i) -> p g u t i", g=4, t=PACK, i=16),
             in_=w4s_raw[:].rearrange("p (g u i t) -> p g u t i", g=4, t=PACK, i=16),
@@ -172,19 +184,18 @@ def tile_list_microfilm_article_linker_kernel(
         gather_words(v_words[0], tab_sb[0], idx, 0, BANK)
         gather_words(v_words[0], tab_sb[0], idx, BANK, S)
 
-        load_page(1)
         load_wgs(1, slice(0, S))
         load_w1(1)
         load_low(0, 1)
         load_words(tab2_sb[0], tab2_words, 0)
         load_words(tab2_sb[1], tab2_words, 1)
-        load_wgs(2, slice(0, S))
         load_wgs(3, slice(0, S))
         with nc.allow_non_contiguous_dma(reason="one factor a partition"):
             nc.sync.dma_start(out=cand_sb[:], in_=cand.rearrange("(c p) -> p c", p=P))
-        for i in range(2, ROW_TILES):
+        load_wgs(2, slice(0, S))
+        for i in range(2, 6):
             load_page(i)
-            load_low(i - 1, 2 if i == ROW_TILES - 1 else 1)
+            load_low(i - 1, 1)
         quantise_w1(1)
 
         def first_product(i):
@@ -236,7 +247,7 @@ def tile_list_microfilm_article_linker_kernel(
             )
 
         def second_pass(b):
-            x_bf = keep.tile([P, NP, PACK], BF16, name="x_bf%d" % b, tag="bf%d" % b, align_bytes=64)
+            x_bf = keep.tile([P, NP, PACK], BF16, name="x_bf%d" % b, align_bytes=64)
             dst = x_bf[:].rearrange("p (c i) t -> p c t i", i=4)
             src = x_planes[b][:].rearrange("p t (c i) -> p c t i", i=4)
             if b == 0:
@@ -263,8 +274,9 @@ def tile_list_microfilm_article_linker_kernel(
             first_product(i)
 
         score = []
-        for u in range(2):
-            part = keep.tile([P, PACK, NP], F32, name="score%d" % u, tag="stage%d" % u)
+
+        def load_score(u):
+            part = shared.tile([P, PACK, NP], F32, name="score%d" % u, offset=AT_PAGE[u])
             nc.sync.dma_start(out=part[:], in_=pagedist.rearrange("(u c p) n -> u p c n", u=2, p=P)[u])
             score.append(part)
 
@@ -278,6 +290,13 @@ def tile_list_microfilm_article_linker_kernel(
                 fetch(i, 0, NP)
             if i <= 2:
                 gather_words(v2_words[i - 1], tab2_sb[i - 1], idx2, 0, S2)
+            if i == 2:
+                load_page(6)
+                load_low(5, 1)
+                load_page(7)
+                load_low(6, 2)
+                load_score(0)
+                load_score(1)
             if i == PACK:
                 second_pass(0)
         last = ROW_TILES - 1

@@ -2,7 +2,7 @@ from contextlib import ExitStack
 
 import concourse.mybir as mybir
 
-K, KA, KB, H, T, S, T2, NP, T3, S2 = 1536, 512, 1024, 1024, 4096, 1024, 2048, 512, 2048, 1024
+K, H, T, S, T2, NP, T3, S2 = 1536, 1024, 4096, 1024, 2048, 512, 2048, 1024
 FLOPS = 2 * K * H * S + 2 * H * S2 * NP
 
 F32 = mybir.dt.float32
@@ -20,21 +20,53 @@ P = 128
 PACK = 4
 BANK = 512
 QUADS = 4
+PER_COLUMN = 16
 ROW_TILES = H // P
-SPLIT = 48
+OUT_TILES = S2 // P
+LAST = ROW_TILES - 1
+STAGE1_BANKS = 4
+FIRST = 256
+SCALAR_SHARE = 48
 
-KIB = 1024
-SLOT = 32
-AT_TAB = {1: 0, 2: 16 * KIB, 0: 32 * KIB}
-AT_WGS = {0: 57600, 1: 0, 2: 12 * KIB + SLOT, 3: 86336 + SLOT}
-AT_W1 = {0: 73984, 1: 4 * KIB}
-AT_PAGE = {0: 49408, 1: 61696, 2: 16416, 3: 24640, 4: 32864, 5: 41120, 6: 69888, 7: 78144}
-AT_LOW = {0: 12 * KIB, 1: 24608, 2: 32832, 3: 41056, 4: 41088, 5: 78080, 6: 78112}
-AT_TAB2 = {0: 69888, 1: 78080}
-AT_TAB_SC = 47104
-AT_W4 = 59648
-AT_W1_BF = 86336
-AT_CAND = 86336
+V_ROWS_AT = (112, 32, 48)
+V_PLANE_FIRST = (12, 0, 0)
+V2_ROWS_AT = (96, 112)
+V2_PLANE_FIRST = (4, 8)
+
+TAB_BYTES, PAGE_BYTES, WGS_BYTES, SLOT = 4 * T, 4 * T2, 4 * S, 32
+AT_TAB = {1: 0, 2: TAB_BYTES, 0: 2 * TAB_BYTES}
+AT_TAB_SCALES = AT_TAB[0] - T // 2
+AT_WGS = {1: 0, 2: WGS_BYTES + PAGE_BYTES + SLOT}
+AT_PAGE = {1: WGS_BYTES, 4: WGS_BYTES + SLOT}
+AT_LOW = {3: WGS_BYTES, 0: WGS_BYTES + PAGE_BYTES + SLOT + WGS_BYTES}
+AT_B = WGS_BYTES + PAGE_BYTES + SLOT + WGS_BYTES + SLOT
+AT_W1_SECOND = AT_B + 2 * (PAGE_BYTES + SLOT)
+AT_WGS3 = AT_W1_SECOND + SLOT + PAGE_BYTES
+AT_CAND = AT_WGS3 + WGS_BYTES
+AT_V2_PLANES = AT_CAND + SLOT
+AT_TAB2 = AT_V2_PLANES + S2
+AT_WGS0 = AT_TAB2 + 2 * PAGE_BYTES + 2 * SLOT
+AT_W4_WORDS = AT_WGS0 - 2 * H
+
+
+def offsets_of_reused_tiles():
+    page = dict(AT_PAGE)
+    page[0] = AT_TAB2 + PAGE_BYTES
+    page[2] = AT_B
+    page[3] = AT_B + PAGE_BYTES + SLOT
+    page[5] = AT_W1_SECOND + SLOT
+    page[6] = AT_TAB2
+    page[7] = AT_TAB2 + PAGE_BYTES + 2 * SLOT
+    factors = dict(AT_WGS)
+    factors[0] = AT_WGS0
+    factors[3] = AT_WGS3
+    floor = dict(AT_LOW)
+    floor[1] = AT_B + PAGE_BYTES
+    floor[2] = AT_B + 2 * PAGE_BYTES + SLOT
+    floor[4] = AT_W1_SECOND
+    floor[5] = AT_TAB2 + PAGE_BYTES
+    floor[6] = AT_TAB2 + PAGE_BYTES + SLOT
+    return page, factors, floor
 
 
 def tile_list_microfilm_article_linker_kernel(
@@ -42,96 +74,188 @@ def tile_list_microfilm_article_linker_kernel(
     tab2_words, tab2_scales, cand, pagedist, offs, offs2, offs3, offs4, out,
 ):
     nc = tc.nc
+    at_page, at_wgs, at_low = offsets_of_reused_tiles()
     with ExitStack() as ctx:
         lists = ctx.enter_context(tc.tile_pool(name="lists", bufs=1))
         keep = ctx.enter_context(tc.tile_pool(name="keep", bufs=1))
-        shared = ctx.enter_context(tc.tile_pool(name="shared", bufs=1))
+        reused = ctx.enter_context(tc.tile_pool(name="reused", bufs=1))
         ring = ctx.enter_context(tc.tile_pool(name="ring", bufs=3))
         psum = ctx.enter_context(tc.psum_pool(name="psum", bufs=1))
 
-        idx = lists.tile([P, S // 16], U16, name="idx")
-        idx2 = lists.tile([P, S2 // 16], U16, name="idx2")
-        idx3 = lists.tile([P, S // 16], U16, name="idx3")
-        idx4 = lists.tile([P, NP // 16], U16, name="idx4")
-        banks = [psum.tile([P, BANK], F32, name="bank%d" % i) for i in range(8)]
+        idx = lists.tile([P, S // PER_COLUMN], U16, name="idx")
+        idx2 = lists.tile([P, S2 // PER_COLUMN], U16, name="idx2")
+        idx3 = lists.tile([P, S // PER_COLUMN], U16, name="idx3")
+        idx4 = lists.tile([P, NP // PER_COLUMN], U16, name="idx4")
+        banks = [psum.tile([P, BANK], F32, name="bank%d" % n) for n in range(OUT_TILES)]
 
-        tab_sb = [shared.tile([P, T], I32, name="tab%d" % a, offset=AT_TAB[a]) for a in range(3)]
-        tab_sc = shared.tile([P, T], U8, name="tab_sc", offset=AT_TAB_SC)
+        tab_sb = [reused.tile([P, T], I32, name="tab%d" % a, offset=AT_TAB[a]) for a in range(3)]
+        tab_sc = reused.tile([P, T], U8, name="tab_sc", offset=AT_TAB_SCALES)
         v_words = [keep.tile([P, S], U32, name="v_words%d" % a, align_bytes=64) for a in range(3)]
-        v_sc_rows = keep.tile([P, S], U8, name="v_sc_rows", align_bytes=64)
-        v_sc = keep.tile([P, 3 * S], U8, name="v_sc", align_bytes=64)
-        w4_raw = shared.tile([P, 2 * 2 * H], U8, name="w4_raw", offset=AT_W4)
+        v_rows = keep.tile([P, S], U8, name="v_rows", align_bytes=64)
+        v_planes = keep.tile([P, 3 * S], U8, name="v_planes", align_bytes=64)
+        w4_raw = reused.tile([P, 2 * 2 * H], U8, name="w4_raw", offset=AT_W4_WORDS)
         w4_sb = keep.tile([P, 2 * 2 * H], U8, name="w4_sb", align_bytes=64)
-        w4s_raw = keep.tile([P, 2 * H], U8, name="w4s_raw", align_bytes=64)
-        w4s_sb = keep.tile([P, 2 * H], U8, name="w4s_sb", align_bytes=64)
-        w1_raw = [shared.tile([P, PACK, BANK], F32, name="w1_raw%d" % b, offset=AT_W1[b]) for b in range(2)]
-        w1_bf = [
-            shared.tile([P, PACK * BANK], BF16, name="w1_bf0", align_bytes=64, offset=AT_W1_BF),
-            keep.tile([P, PACK * BANK], BF16, name="w1_bf1", align_bytes=64),
+        w4_planes_raw = keep.tile([P, 2 * H], U8, name="w4_planes_raw", align_bytes=64)
+        w4_planes = keep.tile([P, 2 * H], U8, name="w4_planes", align_bytes=64)
+        w1_raw = [
+            keep.tile([P, PACK, BANK], F32, name="w1_raw0"),
+            reused.tile([P, PACK, BANK], F32, name="w1_raw1", offset=AT_W1_SECOND),
         ]
-        w1_q = [keep.tile([P, BANK], U32, name="w1_q%d" % b, align_bytes=64) for b in range(2)]
-        w1_sc = [keep.tile([P, BANK], U8, name="w1_sc%d" % b, align_bytes=64) for b in range(2)]
+        w1_bf = [keep.tile([P, PACK * BANK], BF16, name="w1_bf%d" % b, align_bytes=64) for b in range(2)]
+        w1_words = [keep.tile([P, BANK], U32, name="w1_words%d" % b, align_bytes=64) for b in range(2)]
+        w1_planes = [keep.tile([P, BANK], U8, name="w1_planes%d" % b, align_bytes=64) for b in range(2)]
         b1_sb = keep.tile([P, 2, PACK], F32, name="b1_sb")
         gain_sb = keep.tile([P, 2, PACK], F32, name="gain_sb")
-        cand_sb = shared.tile([P, S2 // P], F32, name="cand_sb", offset=AT_CAND)
-        wgs_sb = [shared.tile([P, S], F32, name="wgs%d" % t, offset=AT_WGS[t]) for t in range(PACK)]
-        tab2_sb = [shared.tile([P, T3], I32, name="tab2_%d" % a, offset=AT_TAB2[a]) for a in range(2)]
+        cand_sb = reused.tile([P, OUT_TILES], F32, name="cand_sb", offset=AT_CAND)
+        wgs_sb = [reused.tile([P, S], F32, name="wgs%d" % t, offset=at_wgs[t]) for t in range(PACK)]
+        tab2_sb = [reused.tile([P, T3], I32, name="tab2_%d" % a, offset=AT_TAB2 + a * PAGE_BYTES) for a in range(2)]
         tab2_sc = keep.tile([P, T3], U8, name="tab2_sc")
         v2_words = [keep.tile([P, S2], U32, name="v2_words%d" % a, align_bytes=64) for a in range(2)]
-        v2_sc = keep.tile([P, S2], U8, name="v2_sc", align_bytes=64)
+        v2_rows = keep.tile([P, S2], U8, name="v2_rows", align_bytes=64)
+        v2_planes = reused.tile([P, S2], U8, name="v2_planes", align_bytes=64, offset=AT_V2_PLANES)
+        tanh_sb = [keep.tile([P, BANK], F32, name="tanh%d" % n) for n in range(2)]
         h = [keep.tile([P, S], F32, name="h%d" % i) for i in range(ROW_TILES)]
-        x_planes = [keep.tile([P, PACK, NP], BF16, name="x_planes%d" % b, align_bytes=64) for b in range(2)]
-        x_q = [keep.tile([P, NP], U32, name="x_q%d" % b, align_bytes=64) for b in range(2)]
-        x_sc = [keep.tile([P, NP], U8, name="x_sc%d" % b, align_bytes=64) for b in range(2)]
+        x_rows = [keep.tile([P, PACK, NP], BF16, name="x_rows%d" % b, align_bytes=64) for b in range(2)]
+        x_bf = [keep.tile([P, NP, PACK], BF16, name="x_bf%d" % b, align_bytes=64) for b in range(2)]
+        x_words = [keep.tile([P, NP], U32, name="x_words%d" % b, align_bytes=64) for b in range(2)]
+        x_planes = [keep.tile([P, NP], U8, name="x_planes%d" % b, align_bytes=64) for b in range(2)]
+        pages, low_sb, picked, scores = {}, {}, {}, []
 
-        for plane in (tab_sc[0:80, :], w4s_raw[:], v_sc[:], tab2_sc[:]):
-            nc.vector.memset(plane.bitcast(I32), 0)
+        def entries(offsets, lo, hi):
+            return offsets[:, lo // PER_COLUMN : hi // PER_COLUMN]
+
 
         def load_words(dst, words, a):
             nc.sync.dma_start(out=dst[:], in_=words[a].rearrange("p t i -> p (t i)").bitcast(I32))
-
-        def load_wgs(t, cols):
-            rows = wgs.rearrange("(q t) s -> t q s", t=PACK)[t]
-            for g in (0, 2, 1, 3):
-                nc.sync.dma_start(out=wgs_sb[t][32 * g : 32 * (g + 1), cols], in_=rows[:, cols])
 
         def load_w1(b):
             rows = w1.rearrange("(p j) c -> p j c", j=PACK)
             nc.sync.dma_start(out=w1_raw[b][:], in_=rows[:, :, b * BANK : (b + 1) * BANK])
 
-        pages = []
+        def load_wgs(t, lo, hi):
+            rows = wgs.rearrange("(q t) s -> t q s", t=PACK)[t]
+            for q in (0, 2, 1, 3):
+                nc.sync.dma_start(out=wgs_sb[t][32 * q : 32 * (q + 1), lo:hi], in_=rows[:, lo:hi])
 
         def load_page(i):
             b, t = divmod(i, PACK)
-            page = shared.tile([P, T2], F32, name="page%d" % i, offset=AT_PAGE[i])
-            rows = page0.rearrange("(b p t) n -> b t p n", b=2, t=PACK)[b, t]
-            nc.sync.dma_start(out=page[:], in_=rows)
-            pages.append(page)
-
-        low_sb = {}
+            pages[i] = reused.tile([P, T2], F32, name="page%d" % i, offset=at_page[i])
+            nc.sync.dma_start(out=pages[i][:], in_=page0.rearrange("(b p t) n -> b t p n", b=2, t=PACK)[b, t])
 
         def load_low(i, count):
             b, t = divmod(i, PACK)
-            col = shared.tile([P, count], F32, name="low%d" % i, offset=AT_LOW[i])
-            with nc.allow_non_contiguous_dma(reason="one value a partition"):
-                nc.sync.dma_start(out=col[:], in_=low.rearrange("(b p t) -> b p t", b=2, t=PACK)[b, :, t : t + count])
+            columns = reused.tile([P, count], F32, name="low%d" % i, offset=at_low[i])
+            with nc.allow_non_contiguous_dma(reason="one or two values a partition"):
+                nc.sync.dma_start(
+                    out=columns[:], in_=low.rearrange("(b p t) -> b p t", b=2, t=PACK)[b, :, t : t + count],
+                )
             for j in range(count):
-                low_sb[i + j] = col[:, j : j + 1]
+                low_sb[i + j] = columns[:, j : j + 1]
+
+        def load_scores(u, over_page):
+            part = reused.tile([P, PACK, NP], F32, name="scores%d" % u, offset=at_page[over_page])
+            nc.sync.dma_start(out=part[:], in_=pagedist.rearrange("(u c p) n -> u p c n", u=2, p=P)[u])
+            scores.append(part)
+
+        def move_scale_rows(planes, first, rows, at):
+            for q in range(QUADS):
+                nc.sync.dma_start(
+                    out=planes[32 * q + first : 32 * q + first + 4, :].bitcast(I32),
+                    in_=rows[at + 4 * q : at + 4 * q + 4, :].bitcast(I32),
+                )
+
+
+        def zero(part):
+            nc.vector.memset(part.bitcast(I32), 0)
+
+        def gather_words(dst, table, offsets, lo, hi):
+            nc.vector.tensor_copy(dst[:, lo:hi], table[:].bitcast(U32).indirect(entries(offsets, lo, hi)))
+
+        def deal(dst, src, run):
+            nc.vector.tensor_copy(
+                out=dst.rearrange("p (g t u i) -> p g u t i", g=4, t=PACK, i=run),
+                in_=src.rearrange("p (g u i t) -> p g u t i", g=4, t=PACK, i=run),
+            )
 
         def quantise_w1(b):
             nc.scalar.copy(
                 out=w1_bf[b][:].rearrange("p (t m j) -> p m t j", t=PACK, j=PACK),
                 in_=w1_raw[b][:].rearrange("p j (m t) -> p m t j", t=PACK),
             )
-            nc.vector.quantize_mx(out=w1_q[b][:].bitcast(FP8X4), scales=w1_sc[b][:], in_=w1_bf[b][:])
+            nc.vector.quantize_mx(out=w1_words[b][:].bitcast(FP8X4), scales=w1_planes[b][:], in_=w1_bf[b][:])
 
-        def gather_words(dst, src, offsets, lo, hi):
-            nc.vector.tensor_copy(dst[:, lo:hi], src[:].bitcast(U32).indirect(offsets[:, lo // 16 : hi // 16]))
+        def first_product(i, lo, hi, bank, tanh_tile):
+            b, t = divmod(i, PACK)
+            acc = bank[:, : hi - lo]
+            for a in (1, 2):
+                column = (a - 1) * H + i * P
+                nc.tensor.matmul_mx(
+                    out=acc,
+                    lhsT=w4_sb[:, 2 * column : 2 * (column + P)].bitcast(FP4X4),
+                    lhsT_scale=w4_planes[:, column : column + P],
+                    rhs=v_words[a][:, lo:hi].bitcast(FP8X4),
+                    rhs_scale=v_planes[:, a * S + lo : a * S + hi],
+                    start=(a == 1),
+                    stop=False,
+                )
+            nc.tensor.matmul_mx(
+                out=acc,
+                lhsT=w1_words[b][:, t * P : (t + 1) * P].bitcast(FP8X4),
+                lhsT_scale=w1_planes[b][:, t * P : (t + 1) * P],
+                rhs=v_words[0][:, lo:hi].bitcast(FP8X4),
+                rhs_scale=v_planes[V_PLANE_FIRST[0] : P, lo:hi],
+                start=False,
+                stop=True,
+            )
+            level = tanh_tile[:, : hi - lo]
+            nc.scalar.activation(out=level, in_=acc, func=ACT.Tanh, bias=b1_sb[:, b, t : t + 1])
+            nc.scalar.activation(out=h[i][:, lo:hi], in_=level, func=ACT.Copy, scale=gain_sb[:, b, t : t + 1])
+
+        def put(i, lo, hi):
+            nc.vector.tensor_tensor(
+                pages[i][:].indirect(entries(idx3, lo, hi)), h[i][:, lo:hi], wgs_sb[i % PACK][:, lo:hi], ALU.mult,
+            )
+
+        def fetch(i, lo, hi):
+            if lo == 0:
+                picked[i] = ring.tile([P, NP], F32, name="picked")
+            nc.vector.tensor_copy(picked[i][:, lo:hi], pages[i][:].indirect(entries(idx4, lo, hi)))
+
+        def raise_to_low(i, lo, hi):
+            b, t = divmod(i, PACK)
+            nc.vector.tensor_scalar(
+                out=x_rows[b][:, t, lo:hi], in0=picked[i][:, lo:hi], scalar1=low_sb[i], scalar2=None, op0=ALU.max,
+            )
+
+        def second_product_pass(b, scalar_groups):
+            dst = x_bf[b][:].rearrange("p (c i) t -> p c t i", i=4)
+            src = x_rows[b][:].rearrange("p t (c i) -> p c t i", i=4)
+            nc.scalar.copy(out=dst[:, :scalar_groups], in_=src[:, :scalar_groups])
+            if scalar_groups < NP // 4:
+                nc.vector.tensor_copy(out=dst[:, scalar_groups:], in_=src[:, scalar_groups:])
+            nc.vector.quantize_mx(
+                out=x_words[b][:].bitcast(FP8X4), scales=x_planes[b][:],
+                in_=x_bf[b][:].rearrange("p n t -> p (n t)"),
+            )
+            for c in range(OUT_TILES):
+                columns = slice(c * P, (c + 1) * P)
+                nc.tensor.matmul_mx(
+                    out=banks[c][:],
+                    lhsT=v2_words[b][:, columns].bitcast(FP8X4),
+                    lhsT_scale=v2_planes[V2_PLANE_FIRST[b] : P, columns],
+                    rhs=x_words[b][:].bitcast(FP8X4),
+                    rhs_scale=x_planes[b][:],
+                    start=(b == 0),
+                    stop=(b == 1),
+                )
+
+        for part in (w4_planes_raw[:], tab_sc[0:32, :], tab_sc[64:112, :], v_planes[:], tab2_sc[0:96, :]):
+            zero(part)
 
         scale_rows = tab_scales.bitcast(I32).rearrange("a q n -> (a q) n")
         nc.sync.dma_start(idx[:], offs)
-        nc.sync.dma_start(out=tab_sc[96:128, :].bitcast(I32), in_=scale_rows[16:48, :])
-        nc.sync.dma_start(out=tab_sc[80:96, :].bitcast(I32), in_=scale_rows[0:16, :])
+        nc.sync.dma_start(out=tab_sc[32:64, :].bitcast(I32), in_=scale_rows[16:48, :])
+        nc.sync.dma_start(out=tab_sc[112:128, :].bitcast(I32), in_=scale_rows[0:16, :])
         nc.sync.dma_start(
             out=w4_raw[:].bitcast(I32).rearrange("p (a c) -> p a c", a=2),
             in_=w4_words.bitcast(I32).rearrange("a p c -> p a c"),
@@ -140,174 +264,97 @@ def tile_list_microfilm_article_linker_kernel(
         nc.sync.dma_start(idx3[:], offs3)
         nc.sync.dma_start(idx4[:], offs4)
         load_words(tab_sb[1], tab_words, 1)
+        for vector, dst in ((b1, b1_sb), (gain, gain_sb)):
+            nc.sync.dma_start(out=dst[:], in_=vector.rearrange("(b p t) -> p b t", b=2, t=PACK))
         for q in range(QUADS):
-            nc.gpsimd.dma_start(
-                out=w4s_raw[32 * q : 32 * q + 4, :].bitcast(I32).rearrange("p (a c) -> p a c", a=2),
+            nc.sync.dma_start(
+                out=w4_planes_raw[32 * q : 32 * q + 4, :].bitcast(I32).rearrange("p (a c) -> p a c", a=2),
                 in_=w4_scales[:, 4 * q : 4 * q + 4, :].bitcast(I32).rearrange("a r c -> r a c"),
             )
-        for vec, dst in ((b1, b1_sb), (gain, gain_sb)):
-            nc.gpsimd.dma_start(out=dst[:], in_=vec.rearrange("(b p t) -> p b t", b=2, t=PACK))
-        for q in range(QUADS):
-            nc.gpsimd.dma_start(
-                out=tab2_sc[32 * q : 32 * q + 8, :].bitcast(I32),
-                in_=tab2_scales[:, 4 * q : 4 * q + 4, :].bitcast(I32),
-            )
         load_w1(0)
-        load_words(tab_sb[2], tab_words, 2)
-
-        nc.vector.tensor_copy(v_sc_rows[:], tab_sc[:].indirect(idx[:]))
-        moves = [(a, q) for a in (1, 2, 0) for q in range(QUADS)]
-        for n, (a, q) in enumerate(moves):
-            if n == len(moves) // 2:
-                load_words(tab_sb[0], tab_words, 0)
-            first = 80 + 16 * a + 4 * q
-            nc.sync.dma_start(
-                out=v_sc[32 * q : 32 * q + 4, a * S : (a + 1) * S].bitcast(I32),
-                in_=v_sc_rows[first : first + 4, :].bitcast(I32),
-            )
-        nc.vector.tensor_copy(
-            out=w4_sb[:].bitcast(U16).rearrange("p (g t u i) -> p g u t i", g=4, t=PACK, i=8),
-            in_=w4_raw[:].bitcast(U16).rearrange("p (g u i t) -> p g u t i", g=4, t=PACK, i=8),
+        nc.sync.dma_start(
+            out=tab2_sc[96:128, :].bitcast(I32), in_=tab2_scales.bitcast(I32).rearrange("a q n -> (a q) n"),
         )
+
+        nc.vector.tensor_copy(v_rows[:], tab_sc[:].indirect(idx[:]))
+        for a, following in ((1, 2), (2, 0)):
+            move_scale_rows(v_planes[:, a * S : (a + 1) * S], V_PLANE_FIRST[a], v_rows, V_ROWS_AT[a])
+            load_words(tab_sb[following], tab_words, following)
+        move_scale_rows(v_planes[:, 0:S], V_PLANE_FIRST[0], v_rows, V_ROWS_AT[0])
+        deal(w4_sb[:].bitcast(U16), w4_raw[:].bitcast(U16), 8)
         load_page(0)
-        load_wgs(0, slice(0, S))
-        load_page(1)
+        load_wgs(0, 0, FIRST)
+        load_wgs(0, FIRST, S)
 
-        nc.vector.tensor_copy(
-            out=w4s_sb[:].rearrange("p (g t u i) -> p g u t i", g=4, t=PACK, i=16),
-            in_=w4s_raw[:].rearrange("p (g u i t) -> p g u t i", g=4, t=PACK, i=16),
-        )
+        deal(w4_planes[:], w4_planes_raw[:], 16)
         gather_words(v_words[1], tab_sb[1], idx, 0, S)
         quantise_w1(0)
         gather_words(v_words[2], tab_sb[2], idx, 0, S)
-        nc.vector.tensor_copy(v2_sc[:], tab2_sc[:].indirect(idx2[:]))
+        nc.vector.tensor_copy(v2_rows[:], tab2_sc[:].indirect(idx2[:]))
         gather_words(v_words[0], tab_sb[0], idx, 0, BANK)
         gather_words(v_words[0], tab_sb[0], idx, BANK, S)
 
-        load_wgs(1, slice(0, S))
-        load_w1(1)
+        load_page(1)
+        load_wgs(1, 0, S)
+        load_wgs(2, 0, S)
         load_low(0, 1)
+        load_page(2)
+        load_low(1, 1)
+        load_w1(1)
+        load_wgs(3, 0, S)
+        load_page(3)
+        load_low(2, 1)
         load_words(tab2_sb[0], tab2_words, 0)
-        load_words(tab2_sb[1], tab2_words, 1)
-        load_wgs(3, slice(0, S))
+        zero(v2_planes[:])
+        for a in range(2):
+            move_scale_rows(v2_planes, V2_PLANE_FIRST[a], v2_rows, V2_ROWS_AT[a])
         with nc.allow_non_contiguous_dma(reason="one factor a partition"):
             nc.sync.dma_start(out=cand_sb[:], in_=cand.rearrange("(c p) -> p c", p=P))
-        load_wgs(2, slice(0, S))
-        for i in range(2, 6):
-            load_page(i)
-            load_low(i - 1, 1)
         quantise_w1(1)
 
-        def first_product(i):
-            b, t = divmod(i, PACK)
-            for half in range(2):
-                bank = banks[(2 * i + half) % 8]
-                cols = slice(half * BANK, (half + 1) * BANK)
-                for a in range(2):
-                    c0 = a * H + i * P
-                    nc.tensor.matmul_mx(
-                        out=bank[:],
-                        lhsT=w4_sb[:, 2 * c0 : 2 * (c0 + P)].bitcast(FP4X4),
-                        lhsT_scale=w4s_sb[:, c0 : c0 + P],
-                        rhs=v_words[1 + a][:, cols].bitcast(FP8X4),
-                        rhs_scale=v_sc[:, (1 + a) * S + half * BANK : (1 + a) * S + (half + 1) * BANK],
-                        start=(a == 0),
-                        stop=False,
-                    )
-                nc.tensor.matmul_mx(
-                    out=bank[:],
-                    lhsT=w1_q[b][:, t * P : (t + 1) * P].bitcast(FP8X4),
-                    lhsT_scale=w1_sc[b][:, t * P : (t + 1) * P],
-                    rhs=v_words[0][:, cols].bitcast(FP8X4),
-                    rhs_scale=v_sc[:, cols],
-                    start=False,
-                    stop=True,
-                )
-                level = ring.tile([P, BANK], F32, name="level")
-                nc.scalar.activation(out=level[:], in_=bank[:], func=ACT.Tanh, bias=b1_sb[:, b, t : t + 1])
-                nc.scalar.activation(out=h[i][:, cols], in_=level[:], func=ACT.Copy, scale=gain_sb[:, b, t : t + 1])
+        pieces = [(0, 0, FIRST), (0, FIRST, BANK), (0, BANK, S)]
+        pieces.extend((i, lo, lo + BANK) for i in range(1, ROW_TILES) for lo in (0, BANK))
+        for n, (i, lo, hi) in enumerate(pieces):
+            first_product(i, lo, hi, banks[n % STAGE1_BANKS], tanh_sb[n % 2])
 
-        def put(i, lo, hi):
-            nc.vector.tensor_tensor(
-                pages[i][:].indirect(idx3[:, lo // 16 : hi // 16]),
-                h[i][:, lo:hi], wgs_sb[i % PACK][:, lo:hi], ALU.mult,
-            )
-
-        picked = {}
-
-        def fetch(i, lo, hi):
-            if lo == 0:
-                picked[i] = ring.tile([P, NP], F32, name="picked")
-            nc.vector.tensor_copy(picked[i][:, lo:hi], pages[i][:].indirect(idx4[:, lo // 16 : hi // 16]))
-
-        def raise_to_low(i, lo, hi):
-            b, t = divmod(i, PACK)
-            nc.vector.tensor_scalar(
-                out=x_planes[b][:, t, lo:hi], in0=picked[i][:, lo:hi], scalar1=low_sb[i], scalar2=None, op0=ALU.max,
-            )
-
-        def second_pass(b):
-            x_bf = keep.tile([P, NP, PACK], BF16, name="x_bf%d" % b, align_bytes=64)
-            dst = x_bf[:].rearrange("p (c i) t -> p c t i", i=4)
-            src = x_planes[b][:].rearrange("p t (c i) -> p c t i", i=4)
-            if b == 0:
-                nc.scalar.copy(out=dst, in_=src)
-            else:
-                nc.scalar.copy(out=dst[:, :SPLIT], in_=src[:, :SPLIT])
-                nc.vector.tensor_copy(out=dst[:, SPLIT:], in_=src[:, SPLIT:])
-            nc.vector.quantize_mx(
-                out=x_q[b][:].bitcast(FP8X4), scales=x_sc[b][:], in_=x_bf[:].rearrange("p n t -> p (n t)"),
-            )
-            for c in range(S2 // P):
-                cols = slice(c * P, (c + 1) * P)
-                nc.tensor.matmul_mx(
-                    out=banks[c][:],
-                    lhsT=v2_words[b][:, cols].bitcast(FP8X4),
-                    lhsT_scale=v2_sc[4 * b : P, cols],
-                    rhs=x_q[b][:].bitcast(FP8X4),
-                    rhs_scale=x_sc[b][:],
-                    start=(b == 0),
-                    stop=(b == 1),
-                )
-
-        for i in range(ROW_TILES):
-            first_product(i)
-
-        score = []
-
-        def load_score(u):
-            part = shared.tile([P, PACK, NP], F32, name="score%d" % u, offset=AT_PAGE[u])
-            nc.sync.dma_start(out=part[:], in_=pagedist.rearrange("(u c p) n -> u p c n", u=2, p=P)[u])
-            score.append(part)
-
-        put(0, 0, BANK)
-        put(0, BANK, S)
+        put(0, 0, FIRST)
+        put(0, FIRST, S)
         fetch(0, 0, NP)
-        for i in range(1, ROW_TILES):
+        load_words(tab2_sb[1], tab2_words, 1)
+        put(1, 0, S)
+        raise_to_low(0, 0, NP)
+        fetch(1, 0, NP)
+        for i in (4, 5):
+            load_page(i)
+            load_low(i - 1, 1)
+        for i in (2, 3):
             put(i, 0, S)
             raise_to_low(i - 1, 0, NP)
-            if i < ROW_TILES - 1:
-                fetch(i, 0, NP)
-            if i <= 2:
-                gather_words(v2_words[i - 1], tab2_sb[i - 1], idx2, 0, S2)
-            if i == 2:
-                load_page(6)
-                load_low(5, 1)
-                load_page(7)
-                load_low(6, 2)
-                load_score(0)
-                load_score(1)
-            if i == PACK:
-                second_pass(0)
-        last = ROW_TILES - 1
-        fetch(last, 0, NP // 2)
-        fetch(last, NP // 2, NP)
-        raise_to_low(last, 0, NP // 2)
-        raise_to_low(last, NP // 2, NP)
-        second_pass(1)
+            fetch(i, 0, NP)
+            gather_words(v2_words[i - 2], tab2_sb[i - 2], idx2, 0, S2)
+        load_page(6)
+        load_low(5, 1)
+        load_page(LAST)
+        load_low(6, 2)
+        load_scores(0, 3)
+        put(PACK, 0, S)
+        raise_to_low(PACK - 1, 0, NP)
+        fetch(PACK, 0, NP)
+        load_scores(1, PACK)
+        second_product_pass(0, NP // 4)
+        for i in range(PACK + 1, LAST):
+            put(i, 0, S)
+            raise_to_low(i - 1, 0, NP)
+            fetch(i, 0, NP)
+        put(LAST, 0, S)
+        raise_to_low(LAST - 1, 0, NP)
+        for step in (fetch, raise_to_low):
+            step(LAST, 0, NP // 2)
+            step(LAST, NP // 2, NP)
+        second_product_pass(1, SCALAR_SHARE)
 
-        for c in range(S2 // P):
-            part = score[c // PACK][:, c % PACK, :]
+        for c in range(OUT_TILES):
+            part = scores[c // PACK][:, c % PACK, :]
             nc.vector.scalar_tensor_tensor(
                 out=part, in0=banks[c][:], scalar=cand_sb[:, c : c + 1], in1=part, op0=ALU.mult, op1=ALU.add,
             )

from contextlib import ExitStack

import concourse.mybir as mybir

K, H, T, S, T2, NP, T3, S2 = 1536, 1024, 4096, 1024, 2048, 512, 2048, 1024
FLOPS = 2 * K * H * S + 2 * H * S2 * NP

F32 = mybir.dt.float32
BF16 = mybir.dt.bfloat16
I32 = mybir.dt.int32
U32 = mybir.dt.uint32
U16 = mybir.dt.uint16
U8 = mybir.dt.uint8
FP8X4 = mybir.dt.float8_e4m3fn_x4
FP4X4 = mybir.dt.float4_e2m1fn_x4
ALU = mybir.AluOpType
ACT = mybir.ActivationFunctionType

P = 128
PACK = 4
BANK = 512
QUADS = 4
PER_COLUMN = 16
ROW_TILES = H // P
OUT_TILES = S2 // P
LAST = ROW_TILES - 1
STAGE1_BANKS = 4
FIRST = 256
SCALAR_SHARE = 48

V_ROWS_AT = (112, 32, 48)
V_PLANE_FIRST = (12, 0, 0)
V2_ROWS_AT = (96, 112)
V2_PLANE_FIRST = (4, 8)

TAB_BYTES, PAGE_BYTES, WGS_BYTES, SLOT = 4 * T, 4 * T2, 4 * S, 32
AT_TAB = {1: 0, 2: TAB_BYTES, 0: 2 * TAB_BYTES}
AT_TAB_SCALES = AT_TAB[0] - T // 2
AT_WGS = {1: 0, 2: WGS_BYTES + PAGE_BYTES + SLOT}
AT_PAGE = {1: WGS_BYTES, 4: WGS_BYTES + SLOT}
AT_LOW = {3: WGS_BYTES, 0: WGS_BYTES + PAGE_BYTES + SLOT + WGS_BYTES}
AT_B = WGS_BYTES + PAGE_BYTES + SLOT + WGS_BYTES + SLOT
AT_W1_SECOND = AT_B + 2 * (PAGE_BYTES + SLOT)
AT_WGS3 = AT_W1_SECOND + SLOT + PAGE_BYTES
AT_CAND = AT_WGS3 + WGS_BYTES
AT_V2_PLANES = AT_CAND + SLOT
AT_TAB2 = AT_V2_PLANES + S2
AT_WGS0 = AT_TAB2 + 2 * PAGE_BYTES + 2 * SLOT
AT_W4_WORDS = AT_WGS0 - 2 * H


def offsets_of_reused_tiles():
    page = dict(AT_PAGE)
    page[0] = AT_TAB2 + PAGE_BYTES
    page[2] = AT_B
    page[3] = AT_B + PAGE_BYTES + SLOT
    page[5] = AT_W1_SECOND + SLOT
    page[6] = AT_TAB2
    page[7] = AT_TAB2 + PAGE_BYTES + 2 * SLOT
    factors = dict(AT_WGS)
    factors[0] = AT_WGS0
    factors[3] = AT_WGS3
    floor = dict(AT_LOW)
    floor[1] = AT_B + PAGE_BYTES
    floor[2] = AT_B + 2 * PAGE_BYTES + SLOT
    floor[4] = AT_W1_SECOND
    floor[5] = AT_TAB2 + PAGE_BYTES
    floor[6] = AT_TAB2 + PAGE_BYTES + SLOT
    return page, factors, floor


def tile_list_microfilm_article_linker_kernel(
    tc, tab_words, tab_scales, w1, w4_words, w4_scales, b1, gain, page0, wgs, low,
    tab2_words, tab2_scales, cand, pagedist, offs, offs2, offs3, offs4, out,
):
    nc = tc.nc
    at_page, at_wgs, at_low = offsets_of_reused_tiles()
    with ExitStack() as ctx:
        lists = ctx.enter_context(tc.tile_pool(name="lists", bufs=1))
        keep = ctx.enter_context(tc.tile_pool(name="keep", bufs=1))
        reused = ctx.enter_context(tc.tile_pool(name="reused", bufs=1))
        ring = ctx.enter_context(tc.tile_pool(name="ring", bufs=3))
        psum = ctx.enter_context(tc.psum_pool(name="psum", bufs=1))

        idx = lists.tile([P, S // PER_COLUMN], U16, name="idx")
        idx2 = lists.tile([P, S2 // PER_COLUMN], U16, name="idx2")
        idx3 = lists.tile([P, S // PER_COLUMN], U16, name="idx3")
        idx4 = lists.tile([P, NP // PER_COLUMN], U16, name="idx4")
        banks = [psum.tile([P, BANK], F32, name="bank%d" % n) for n in range(OUT_TILES)]

        tab_sb = [reused.tile([P, T], I32, name="tab%d" % a, offset=AT_TAB[a]) for a in range(3)]
        tab_sc = reused.tile([P, T], U8, name="tab_sc", offset=AT_TAB_SCALES)
        v_words = [keep.tile([P, S], U32, name="v_words%d" % a, align_bytes=64) for a in range(3)]
        v_rows = keep.tile([P, S], U8, name="v_rows", align_bytes=64)
        v_planes = keep.tile([P, 3 * S], U8, name="v_planes", align_bytes=64)
        w4_raw = reused.tile([P, 2 * 2 * H], U8, name="w4_raw", offset=AT_W4_WORDS)
        w4_sb = keep.tile([P, 2 * 2 * H], U8, name="w4_sb", align_bytes=64)
        w4_planes_raw = keep.tile([P, 2 * H], U8, name="w4_planes_raw", align_bytes=64)
        w4_planes = keep.tile([P, 2 * H], U8, name="w4_planes", align_bytes=64)
        w1_raw = [
            keep.tile([P, PACK, BANK], F32, name="w1_raw0"),
            reused.tile([P, PACK, BANK], F32, name="w1_raw1", offset=AT_W1_SECOND),
        ]
        w1_bf = [keep.tile([P, PACK * BANK], BF16, name="w1_bf%d" % b, align_bytes=64) for b in range(2)]
        w1_words = [keep.tile([P, BANK], U32, name="w1_words%d" % b, align_bytes=64) for b in range(2)]
        w1_planes = [keep.tile([P, BANK], U8, name="w1_planes%d" % b, align_bytes=64) for b in range(2)]
        b1_sb = keep.tile([P, 2, PACK], F32, name="b1_sb")
        gain_sb = keep.tile([P, 2, PACK], F32, name="gain_sb")
        cand_sb = reused.tile([P, OUT_TILES], F32, name="cand_sb", offset=AT_CAND)
        wgs_sb = [reused.tile([P, S], F32, name="wgs%d" % t, offset=at_wgs[t]) for t in range(PACK)]
        tab2_sb = [reused.tile([P, T3], I32, name="tab2_%d" % a, offset=AT_TAB2 + a * PAGE_BYTES) for a in range(2)]
        tab2_sc = keep.tile([P, T3], U8, name="tab2_sc")
        v2_words = [keep.tile([P, S2], U32, name="v2_words%d" % a, align_bytes=64) for a in range(2)]
        v2_rows = keep.tile([P, S2], U8, name="v2_rows", align_bytes=64)
        v2_planes = reused.tile([P, S2], U8, name="v2_planes", align_bytes=64, offset=AT_V2_PLANES)
        tanh_sb = [keep.tile([P, BANK], F32, name="tanh%d" % n) for n in range(2)]
        h = [keep.tile([P, S], F32, name="h%d" % i) for i in range(ROW_TILES)]
        x_rows = [keep.tile([P, PACK, NP], BF16, name="x_rows%d" % b, align_bytes=64) for b in range(2)]
        x_bf = [keep.tile([P, NP, PACK], BF16, name="x_bf%d" % b, align_bytes=64) for b in range(2)]
        x_words = [keep.tile([P, NP], U32, name="x_words%d" % b, align_bytes=64) for b in range(2)]
        x_planes = [keep.tile([P, NP], U8, name="x_planes%d" % b, align_bytes=64) for b in range(2)]
        pages, low_sb, picked, scores = {}, {}, {}, []

        def entries(offsets, lo, hi):
            return offsets[:, lo // PER_COLUMN : hi // PER_COLUMN]


        def load_words(dst, words, a):
            nc.sync.dma_start(out=dst[:], in_=words[a].rearrange("p t i -> p (t i)").bitcast(I32))

        def load_w1(b):
            rows = w1.rearrange("(p j) c -> p j c", j=PACK)
            nc.sync.dma_start(out=w1_raw[b][:], in_=rows[:, :, b * BANK : (b + 1) * BANK])

        def load_wgs(t, lo, hi):
            rows = wgs.rearrange("(q t) s -> t q s", t=PACK)[t]
            for q in (0, 2, 1, 3):
                nc.sync.dma_start(out=wgs_sb[t][32 * q : 32 * (q + 1), lo:hi], in_=rows[:, lo:hi])

        def load_page(i):
            b, t = divmod(i, PACK)
            pages[i] = reused.tile([P, T2], F32, name="page%d" % i, offset=at_page[i])
            nc.sync.dma_start(out=pages[i][:], in_=page0.rearrange("(b p t) n -> b t p n", b=2, t=PACK)[b, t])

        def load_low(i, count):
            b, t = divmod(i, PACK)
            columns = reused.tile([P, count], F32, name="low%d" % i, offset=at_low[i])
            with nc.allow_non_contiguous_dma(reason="one or two values a partition"):
                nc.sync.dma_start(
                    out=columns[:], in_=low.rearrange("(b p t) -> b p t", b=2, t=PACK)[b, :, t : t + count],
                )
            for j in range(count):
                low_sb[i + j] = columns[:, j : j + 1]

        def load_scores(u, over_page):
            part = reused.tile([P, PACK, NP], F32, name="scores%d" % u, offset=at_page[over_page])
            nc.sync.dma_start(out=part[:], in_=pagedist.rearrange("(u c p) n -> u p c n", u=2, p=P)[u])
            scores.append(part)

        def move_scale_rows(planes, first, rows, at):
            for q in range(QUADS):
                nc.sync.dma_start(
                    out=planes[32 * q + first : 32 * q + first + 4, :].bitcast(I32),
                    in_=rows[at + 4 * q : at + 4 * q + 4, :].bitcast(I32),
                )


        def zero(part):
            nc.vector.memset(part.bitcast(I32), 0)

        def gather_words(dst, table, offsets, lo, hi):
            nc.vector.tensor_copy(dst[:, lo:hi], table[:].bitcast(U32).indirect(entries(offsets, lo, hi)))

        def deal(dst, src, run):
            nc.vector.tensor_copy(
                out=dst.rearrange("p (g t u i) -> p g u t i", g=4, t=PACK, i=run),
                in_=src.rearrange("p (g u i t) -> p g u t i", g=4, t=PACK, i=run),
            )

        def quantise_w1(b):
            nc.scalar.copy(
                out=w1_bf[b][:].rearrange("p (t m j) -> p m t j", t=PACK, j=PACK),
                in_=w1_raw[b][:].rearrange("p j (m t) -> p m t j", t=PACK),
            )
            nc.vector.quantize_mx(out=w1_words[b][:].bitcast(FP8X4), scales=w1_planes[b][:], in_=w1_bf[b][:])

        def first_product(i, lo, hi, bank, tanh_tile):
            b, t = divmod(i, PACK)
            acc = bank[:, : hi - lo]
            for a in (1, 2):
                column = (a - 1) * H + i * P
                nc.tensor.matmul_mx(
                    out=acc,
                    lhsT=w4_sb[:, 2 * column : 2 * (column + P)].bitcast(FP4X4),
                    lhsT_scale=w4_planes[:, column : column + P],
                    rhs=v_words[a][:, lo:hi].bitcast(FP8X4),
                    rhs_scale=v_planes[:, a * S + lo : a * S + hi],
                    start=(a == 1),
                    stop=False,
                )
            nc.tensor.matmul_mx(
                out=acc,
                lhsT=w1_words[b][:, t * P : (t + 1) * P].bitcast(FP8X4),
                lhsT_scale=w1_planes[b][:, t * P : (t + 1) * P],
                rhs=v_words[0][:, lo:hi].bitcast(FP8X4),
                rhs_scale=v_planes[V_PLANE_FIRST[0] : P, lo:hi],
                start=False,
                stop=True,
            )
            level = tanh_tile[:, : hi - lo]
            nc.scalar.activation(out=level, in_=acc, func=ACT.Tanh, bias=b1_sb[:, b, t : t + 1])
            nc.scalar.activation(out=h[i][:, lo:hi], in_=level, func=ACT.Copy, scale=gain_sb[:, b, t : t + 1])

        def put(i, lo, hi):
            nc.vector.tensor_tensor(
                pages[i][:].indirect(entries(idx3, lo, hi)), h[i][:, lo:hi], wgs_sb[i % PACK][:, lo:hi], ALU.mult,
            )

        def fetch(i, lo, hi):
            if lo == 0:
                picked[i] = ring.tile([P, NP], F32, name="picked")
            nc.vector.tensor_copy(picked[i][:, lo:hi], pages[i][:].indirect(entries(idx4, lo, hi)))

        def raise_to_low(i, lo, hi):
            b, t = divmod(i, PACK)
            nc.vector.tensor_scalar(
                out=x_rows[b][:, t, lo:hi], in0=picked[i][:, lo:hi], scalar1=low_sb[i], scalar2=None, op0=ALU.max,
            )

        def second_product_pass(b, scalar_groups):
            dst = x_bf[b][:].rearrange("p (c i) t -> p c t i", i=4)
            src = x_rows[b][:].rearrange("p t (c i) -> p c t i", i=4)
            nc.scalar.copy(out=dst[:, :scalar_groups], in_=src[:, :scalar_groups])
            if scalar_groups < NP // 4:
                nc.vector.tensor_copy(out=dst[:, scalar_groups:], in_=src[:, scalar_groups:])
            nc.vector.quantize_mx(
                out=x_words[b][:].bitcast(FP8X4), scales=x_planes[b][:],
                in_=x_bf[b][:].rearrange("p n t -> p (n t)"),
            )
            for c in range(OUT_TILES):
                columns = slice(c * P, (c + 1) * P)
                nc.tensor.matmul_mx(
                    out=banks[c][:],
                    lhsT=v2_words[b][:, columns].bitcast(FP8X4),
                    lhsT_scale=v2_planes[V2_PLANE_FIRST[b] : P, columns],
                    rhs=x_words[b][:].bitcast(FP8X4),
                    rhs_scale=x_planes[b][:],
                    start=(b == 0),
                    stop=(b == 1),
                )

        for part in (w4_planes_raw[:], tab_sc[0:32, :], tab_sc[64:112, :], v_planes[:], tab2_sc[0:96, :]):
            zero(part)

        scale_rows = tab_scales.bitcast(I32).rearrange("a q n -> (a q) n")
        nc.sync.dma_start(idx[:], offs)
        nc.sync.dma_start(out=tab_sc[32:64, :].bitcast(I32), in_=scale_rows[16:48, :])
        nc.sync.dma_start(out=tab_sc[112:128, :].bitcast(I32), in_=scale_rows[0:16, :])
        nc.sync.dma_start(
            out=w4_raw[:].bitcast(I32).rearrange("p (a c) -> p a c", a=2),
            in_=w4_words.bitcast(I32).rearrange("a p c -> p a c"),
        )
        nc.sync.dma_start(idx2[:], offs2)
        nc.sync.dma_start(idx3[:], offs3)
        nc.sync.dma_start(idx4[:], offs4)
        load_words(tab_sb[1], tab_words, 1)
        for vector, dst in ((b1, b1_sb), (gain, gain_sb)):
            nc.sync.dma_start(out=dst[:], in_=vector.rearrange("(b p t) -> p b t", b=2, t=PACK))
        for q in range(QUADS):
            nc.sync.dma_start(
                out=w4_planes_raw[32 * q : 32 * q + 4, :].bitcast(I32).rearrange("p (a c) -> p a c", a=2),
                in_=w4_scales[:, 4 * q : 4 * q + 4, :].bitcast(I32).rearrange("a r c -> r a c"),
            )
        load_w1(0)
        nc.sync.dma_start(
            out=tab2_sc[96:128, :].bitcast(I32), in_=tab2_scales.bitcast(I32).rearrange("a q n -> (a q) n"),
        )

        nc.vector.tensor_copy(v_rows[:], tab_sc[:].indirect(idx[:]))
        for a, following in ((1, 2), (2, 0)):
            move_scale_rows(v_planes[:, a * S : (a + 1) * S], V_PLANE_FIRST[a], v_rows, V_ROWS_AT[a])
            load_words(tab_sb[following], tab_words, following)
        move_scale_rows(v_planes[:, 0:S], V_PLANE_FIRST[0], v_rows, V_ROWS_AT[0])
        deal(w4_sb[:].bitcast(U16), w4_raw[:].bitcast(U16), 8)
        load_page(0)
        load_wgs(0, 0, FIRST)
        load_wgs(0, FIRST, S)

        deal(w4_planes[:], w4_planes_raw[:], 16)
        gather_words(v_words[1], tab_sb[1], idx, 0, S)
        quantise_w1(0)
        gather_words(v_words[2], tab_sb[2], idx, 0, S)
        nc.vector.tensor_copy(v2_rows[:], tab2_sc[:].indirect(idx2[:]))
        gather_words(v_words[0], tab_sb[0], idx, 0, BANK)
        gather_words(v_words[0], tab_sb[0], idx, BANK, S)

        load_page(1)
        load_wgs(1, 0, S)
        load_wgs(2, 0, S)
        load_low(0, 1)
        load_page(2)
        load_low(1, 1)
        load_w1(1)
        load_wgs(3, 0, S)
        load_page(3)
        load_low(2, 1)
        load_words(tab2_sb[0], tab2_words, 0)
        zero(v2_planes[:])
        for a in range(2):
            move_scale_rows(v2_planes, V2_PLANE_FIRST[a], v2_rows, V2_ROWS_AT[a])
        with nc.allow_non_contiguous_dma(reason="one factor a partition"):
            nc.sync.dma_start(out=cand_sb[:], in_=cand.rearrange("(c p) -> p c", p=P))
        quantise_w1(1)

        pieces = [(0, 0, FIRST), (0, FIRST, BANK), (0, BANK, S)]
        pieces.extend((i, lo, lo + BANK) for i in range(1, ROW_TILES) for lo in (0, BANK))
        for n, (i, lo, hi) in enumerate(pieces):
            first_product(i, lo, hi, banks[n % STAGE1_BANKS], tanh_sb[n % 2])

        put(0, 0, FIRST)
        put(0, FIRST, S)
        fetch(0, 0, NP)
        load_words(tab2_sb[1], tab2_words, 1)
        put(1, 0, S)
        raise_to_low(0, 0, NP)
        fetch(1, 0, NP)
        for i in (4, 5):
            load_page(i)
            load_low(i - 1, 1)
        for i in (2, 3):
            put(i, 0, S)
            raise_to_low(i - 1, 0, NP)
            fetch(i, 0, NP)
            gather_words(v2_words[i - 2], tab2_sb[i - 2], idx2, 0, S2)
        load_page(6)
        load_low(5, 1)
        load_page(LAST)
        load_low(6, 2)
        load_scores(0, 3)
        put(PACK, 0, S)
        raise_to_low(PACK - 1, 0, NP)
        fetch(PACK, 0, NP)
        load_scores(1, PACK)
        second_product_pass(0, NP // 4)
        for i in range(PACK + 1, LAST):
            put(i, 0, S)
            raise_to_low(i - 1, 0, NP)
            fetch(i, 0, NP)
        put(LAST, 0, S)
        raise_to_low(LAST - 1, 0, NP)
        for step in (fetch, raise_to_low):
            step(LAST, 0, NP // 2)
            step(LAST, NP // 2, NP)
        second_product_pass(1, SCALAR_SHARE)

        for c in range(OUT_TILES):
            part = scores[c // PACK][:, c % PACK, :]
            nc.vector.scalar_tensor_tensor(
                out=part, in0=banks[c][:], scalar=cand_sb[:, c : c + 1], in1=part, op0=ALU.mult, op1=ALU.add,
            )
            nc.sync.dma_start(out=out[c * P : (c + 1) * P, :], in_=part)
